import numpy as np, ml_dtypes
CORES = [88,96,104,112,120,216,224,232,240,248]
N = 10
R, T, B = 8192, 4096, 512
def entries(a): return a.T.reshape(-1)
def pack(v, P): return np.ascontiguousarray(np.asarray(v, np.int32).reshape(-1, P).T)
def lists(rng, how):
    I = rng.integers(0, N * R, (N, T)); E = np.sort(rng.integers(0, T + 1, (N, B)), axis=1)
    if how == "void":
        E = np.zeros((N, B), np.int64)
        for r in range(N): k = np.sort(1 + rng.permutation(B - 2)[:6]); c = np.sort(1 + rng.permutation(T)[:6]); E[r] = np.concatenate([[0], c])[np.searchsorted(k, np.arange(B), side="right")]
        E[rng.integers(N)] = 0
    if how == "one":
        p = rng.permutation(N); z = rng.integers(0, B, N); z[p[0]] = 0; z[p[1]] = B - 1; E = np.where(np.arange(B)[None, :] < z[:, None], 0, T)
        I[p[::2]] = R * p[1] + I[p[::2]] % R
    if how == "single": E = np.broadcast_to(1 + np.arange(B), (N, B)).copy()
    if how == "hotrank": I = R * int(rng.integers(N)) + rng.integers(0, R, (N, T))
    if how == "edge": I = R * rng.integers(0, N, (N, T)) + np.where(rng.random((N, T)) < 0.5, 0, R - 1); E[:, -1] = T
    return {"idx": np.stack([pack(i, 16) for i in I]), "end": np.stack([pack(v, 16) for v in E])}
def setup_inputs(rng):
    return dict({"tab": rng.standard_normal((N, 128, R), dtype=np.float32).astype(ml_dtypes.bfloat16)}, **lists(rng, "uniform"))
def setup_inputs_edge(rng):
    d = setup_inputs(rng); d.update(lists(rng, "edge"))
    for k in ("tab",): d[k] = (d[k].astype(np.float32) * 1048576.0).astype(d[k].dtype)
    return d
def setup_inputs_hotrank(rng):
    d = setup_inputs(rng); d.update(lists(rng, "hotrank"))
    for k in ("tab",): d[k] = (d[k].astype(np.float32) * (1 / 1024.0)).astype(d[k].dtype)
    return d
def setup_inputs_one(rng):
    d = setup_inputs(rng); d.update(lists(rng, "one"))
    return d
def setup_inputs_single(rng):
    d = setup_inputs(rng); d.update(lists(rng, "single"))
    return d
def setup_inputs_void(rng):
    d = setup_inputs(rng); d.update(lists(rng, "void"))
    return d
def check_inputs(x):
    bad = []
    if x["idx"].min() < 0 or x["idx"].max() >= N * R: bad.append("idx out of range")
    if x["end"].min() < 0 or x["end"].max() >= T + 1: bad.append("end out of range")
    if any((np.diff(entries(a)) < 0).any() for a in x["end"]): bad.append("end falls")
    t = x["tab"].astype(np.float32)
    if t.min() < -1e30 or t.max() > 1e30: bad.append("tab beyond -1e30 to 1e30")
    return bad
def reference(tab, idx, end):
    A = np.concatenate(list(tab), axis=1)
    y = np.zeros((N, 128, B), tab.dtype)
    for r in range(N):
        G = A[:, entries(idx[r])]; c = np.concatenate([[0], entries(end[r])])
        for b in range(B):
            if c[b + 1] > c[b]: y[r][:, b] = G[:, c[b]:c[b + 1]].max(axis=1)
    return {"y": y}

@@ -1,0 +1,468 @@
+from concourse.bass import DstId, RemoteDMATransfer
+from concourse.mybir import AluOpType, ActivationFunctionType
+
+R = 8192
+LIST = 4096
+BAGS = 512
+GR = 16
+NB = 8
+PAD = 8
+WIN = R + 2 * PAD
+QU = LIST // 4
+DA = LIST + 8
+FA = DA + BAGS
+DN, DZ = QU + 8, QU + 16 + BAGS
+FB = DZ + BAGS
+ZB = DZ - 8
+IW, EW, QW = LIST // 16, BAGS // 16, QU // 16
+OW = IW + QW
+EF = BAGS // 128
+BIG = 9.9999e29
+WHOLE = 8
+NCORES = 256
+FOLD_MAX = 2
+DEEP_TAB, DEEP_WIN = 2, 3
+ROLES = ["back0", "back1", "aux", "far1", "near1", "far0", "near0", "root"]
+EARLY = 3
+POSTS = {"i": ("near0", "far0"), "e": ("near1", "far1")}
+RELAY = {"back0": "far0", "back1": "far1", "aux": "near0", "root": "near1"}
+
+SCRATCH = {
+    "win": ("sbuf", [128, WIN], "bfloat16"),
+    "flag": ("sbuf", [128, FA + FB], "bfloat16"),
+    "got": ("sbuf", [128, LIST + QU], "bfloat16"),
+    "run": ("sbuf", [128, FA + FB], "bfloat16"),
+    "part": ("sbuf", [128, 2 * BAGS], "bfloat16"),
+    "neg": ("sbuf", [128, BAGS], "bfloat16"),
+    "lt": ("sbuf", [128, OW], "int32"),
+    "off": ("sbuf", [128, OW], "uint16"),
+    "foff": ("sbuf", [128, 2 * EW], "uint16"),
+    "xoff": ("sbuf", [128, 2 * EW], "uint16"),
+    "eq": ("sbuf", [16, EW], "int32"),
+    "pq": ("sbuf", [16, EW], "int32"),
+    "ev": ("sbuf", [16, 4 * EW], "int32"),
+    "pv": ("sbuf", [16, 4 * EW], "int32"),
+    "dq": ("sbuf", [16, 4 * EW], "int32"),
+    "zq": ("sbuf", [16, EW], "int32"),
+    "lo": ("sbuf", [16, 4 * EW], "int32"),
+    "lq": ("sbuf", [16, 4 * EW], "int32"),
+    "fq": ("sbuf", [16, 4 * EW], "uint16"),
+    "blk": ("dram", [NB, 128, R * GR // 128], "bfloat16"),
+    "wsrc": ("dram", [128, R * GR // 128], "bfloat16"),
+    "sti": ("dram", [128, 32], "int32"),
+    "fwi": ("dram", [128, 32], "int32"),
+    "img": ("dram", [10, 128, 32], "int32"),
+    "ste": ("dram", [128, EF], "int32"),
+    "fwe": ("dram", [128, EF], "int32"),
+    "ena": ("dram", [128, 4], "uint16"),
+    "enb": ("dram", [128, 16], "uint16"),
+    "ea": ("dram", [8, 128, 4], "uint16"),
+    "eb": ("dram", [2, 128, 16], "uint16"),
+    "pa": ("dram", [8, 128, 64], "bfloat16"),
+    "pb": ("dram", [8, 128, 64], "bfloat16"),
+    "rl": ("dram", [10, 128, 64], "bfloat16"),
+    "fl": ("dram", [10, 128, 64], "bfloat16"),
+    "fr": ("dram", [10, 128, 64], "bfloat16"),
+    "yd": ("dram", [NB, 128, 64], "bfloat16"),
+}
+SEMAPHORES = (["ld%d" % c for c in range(NB - 1)] + ["wl%d" % c for c in range(8)] + ["yd%d" % c for c in range(NB)]
+              + ["wb", "ls", "lw", "own", "ist", "est", "ero", "fwi", "fwe", "il", "irp", "ea", "eb", "erA", "erB", "of",
+                 "rlA", "rlB", "fl", "fr", "iot", "vm", "vs", "pf", "stA", "stB", "yst"] + ["u%d" % k for k in range(12)])
+PIECES = [(512, "V"), (1088, "S"), (1024, "S"), (896, "S"), (576, "S")]
+PIECES_EARLY = [(1152, "S"), (1088, "S"), (1088, "S"), (768, "S")]
+PLANS = {}
+
+
+def bits(mask):
+    return bin(mask).count("1")
+
+
+def split_mask(mask, k):
+    eng = [1 << i for i in range(16) if mask >> i & 1]
+    n = 1
+    while n * 2 * k <= len(eng):
+        n *= 2
+    return [sum(eng[j * n:(j + 1) * n]) for j in range(k)]
+
+
+def make_plan(T, topo):
+    if "p" in PLANS:
+        return PLANS["p"]
+    cores = list(T.cores)
+    n = len(cores)
+    same_chip = lambda a, b: topo.host(a) == topo.host(b) and topo.chip(a) == topo.chip(b)
+    team = []
+    for c in cores:
+        mine = [d for d in range(NCORES) if same_chip(c, d)]
+        abroad = [d for d in range(NCORES) if not same_chip(c, d) and not topo.same_plane(c, d)][0]
+        port = [d for d in mine if topo.may_write(d, abroad)]
+        here = [d for d in mine if topo.die(d) == topo.die(c) and d != c]
+        there = [d for d in mine if topo.die(d) != topo.die(c)]
+        t = {"root": c, "aux": [d for d in here if d not in port][0]}
+        for nm, ds in (("near", [d for d in here if d in port]), ("far", [d for d in there if d in port]),
+                       ("back", [d for d in there if d not in port])):
+            for k, d in enumerate(ds):
+                t["%s%d" % (nm, k)] = d
+        team.append(t)
+    place = {}
+    for o in range(n):
+        for k, r in enumerate(ROLES):
+            place[team[o][r]] = (o, k)
+    heard = {}
+
+    def common(src, ds):
+        m = 0xFFFF
+        for d in ds:
+            m &= topo.mask(src, d)
+        return m
+
+    def masks(src, dsts):
+        away = [j for j, d in enumerate(dsts) if not same_chip(src, d)]
+        home = [j for j in range(len(dsts)) if j not in away]
+        base = common(src, [dsts[j] for j in away])
+        rest = common(src, [dsts[j] for j in home])
+        if away:
+            rest &= ~base
+        out = {}
+        for js, m in ((away, base), (home, rest)):
+            if js:
+                for j, one in zip(js, split_mask(m, len(js))):
+                    out[j] = one
+        return [out[j] for j in range(len(dsts))]
+
+    posts = {}
+    for q in range(n):
+        t = team[q]
+        for kind in "ie":
+            for j in range(2):
+                src, other = t[POSTS[kind][j]], t[POSTS[kind][1 - j]]
+                m = common(t["root"], [src, other])
+                heard[(src, "fw" + kind)] = bits(m)
+                if kind == "i":
+                    ds = [team[o][POSTS[kind][j]] for o in range(n) if o != q]
+                    sem = "il"
+                else:
+                    ds = [d for d in place if topo.die(d) == topo.die(src) and d != src] + [other]
+                    sem = "ea" if q < WHOLE else "eb"
+                k = -(-len(ds) // 16)
+                posts[src] = (kind, q, list(zip(split_mask(common(src, ds), k), [ds[a::k] for a in range(k)])))
+                for m, some in posts[src][2]:
+                    for d in some:
+                        heard[(d, sem)] = heard.get((d, sem), 0) + bits(m)
+    out = {}
+    for d in place:
+        o, k = place[d]
+        r = ROLES[k]
+        for p, qs in (("A", range(WHOLE)), ("B", range(WHOLE, n))):
+            sends, later = [], []
+            for q in qs:
+                to = (team[q]["aux"], "fr", o, "fr") if r == "root" else (team[q][r], "fl", o, "fl")
+                if to[0] == d:
+                    continue
+                if topo.may_write(d, to[0]):
+                    sends.append((q,) + to)
+                else:
+                    sends.append((q, team[o][RELAY[r]], "rl", q, "rl" + p))
+                    later.append((q,) + to)
+            out[(d, p)] = [(m,) + s for m, s in zip(masks(d, [s[1] for s in sends]), sends)]
+            if later:
+                via = team[o][RELAY[r]]
+                out[(via, "r" + p)] = [(m,) + s for m, s in zip(masks(via, [s[1] for s in later]), later)]
+    for key in out:
+        for m, q, to, buf, slot, sem in out[key]:
+            heard[(to, sem)] = heard.get((to, sem), 0) + bits(m)
+    PLANS["p"] = {"cores": cores, "n": n, "team": team, "place": place, "posts": posts, "out": out, "heard": heard,
+                  "common": common}
+    return PLANS["p"]
+
+
+def rank_program(g, core, T, topo):
+    P = make_plan(T, topo)
+    if core not in P["place"]:
+        return
+    cores, n = P["cores"], P["n"]
+    owner, block = P["place"][core]
+    role = ROLES[block]
+    team = P["team"][owner]
+    root = team["root"]
+    is_root = core == root
+    early = block < EARLY
+    V, S, Y = g.vector, g.scalar, g.sync
+    queues = {"g": g, "v": V, "s": S, "y": Y}
+    total, seen, top = {}, {}, {}
+    fresh = [0]
+
+    def inc(call, sem, k):
+        call.then_inc(T.sem[sem], k)
+        total[sem] = total.get(sem, 0) + k
+        return (sem, total[sem])
+
+    def unique():
+        fresh[0] += 1
+        return "u%d" % (fresh[0] - 1)
+
+    def wait(q, sem, val):
+        if seen.get((q, sem), 0) >= val:
+            return
+        seen[(q, sem)] = val
+        top[sem] = max(top.get(sem, 0), val)
+        queues[q].wait_ge(T.sem[sem], val)
+
+    def hear(q, sem, val=None):
+        total[sem] = P["heard"][(core, sem)] if val is None else val
+        wait(q, sem, total[sem])
+
+    def vsync():
+        if total.get("vs", 0):
+            wait("v", "vs", total["vs"])
+
+    def dst_id(d):
+        rid, pid = topo.addr(d, core)
+        return DstId(rid=rid, pnc=pid)
+
+    def fused(items, local="ls"):
+        tr = []
+        for m, ds, sem, srcs, dsts in items:
+            tr.append(RemoteDMATransfer(dst_ids=[dst_id(d) for d in ds], dma_engine_mask=m, remote_sem=T.sem[sem],
+                                        srcs=srcs, dsts=dsts, alu_op=FOLD_MAX if len(srcs) > 1 else 0))
+            total[local] = total.get(local, 0) + bits(m)
+        g.remote_dma_fused(tr, local_sem=T.sem[local])
+
+    common = lambda ds: P["common"](core, ds)
+
+    if is_root:
+        inc(S.dma_start(T.ste[:], T.end[:]), "est", 16)
+        if owner < WHOLE:
+            inc(Y.dma_start(T.sti[:], T.idx[:]), "ist", 16)
+        else:
+            for j in range(4):
+                inc(Y.dma_start(T.sti[32 * j:32 * j + 32, :], T.idx[:, QW * j:QW * j + QW]), "ist", 16)
+        for k in range(NB - 1):
+            if k >= DEEP_TAB:
+                wait("y", "ld%d" % (k - DEEP_TAB), 16)
+            inc(Y.dma_start(T.blk[k], T.tab[GR * k:GR * k + GR, :]), "ld%d" % k, 16)
+        for kind, src, dst in (("e", T.ste, T.fwe), ("i", T.sti, T.fwi)):
+            wait("g", kind + "st", total[kind + "st"])
+            ds = [team[r] for r in POSTS[kind]]
+            fused([(common(ds), ds, "fw" + kind, [src[:]], [dst[:] for d in ds])])
+        for k in range(NB - 1):
+            wait("g", "ld%d" % k, 16)
+            d = team[ROLES[k]]
+            fused([(topo.mask(core, d), [d], "wb", [T.blk[k]], [T.wsrc[:]])], "lw" if k == NB - 2 else "ls")
+
+    kind = P["posts"][core][0] if core in P["posts"] else ""
+    if kind == "e":
+        whole = owner < WHOLE
+        inc(V.memset(T.pq[0:1, :], 0), "vm", 1)
+        if whole:
+            inc(g.iota(T.dq[:, 0:EW], [[1, EW]], DA, EW), "iot", 1)
+        else:
+            inc(g.iota(T.dq[:], [[QU, 4], [1, EW]], DN, EW), "iot", 1)
+            inc(g.iota(T.zq[:], [[1, EW]], DZ, EW), "iot", 1)
+            inc(g.iota(T.lo[:], [[QU, 4], [0, EW]], 0, 0), "iot", 1)
+        hear("s", "fwe")
+        inc(S.dma_start(T.eq[:], T.fwe[:]), "est", 16)
+        inc(S.dma_start(T.pq[1:16, :], T.fwe[0:120, :]), "est", 16)
+        wait("s", "vm", 1)
+        inc(S.dma_start(T.pq[0:1, 1:EW - EF + 1], T.fwe[120:127, :]), "est", 16)
+        inc(S.dma_start(T.pq[0:1, EW - EF + 1:EW], T.fwe[127:128, 0:EF - 1]), "est", 16)
+        wait("v", "vm", 1)
+        wait("v", "iot", total["iot"])
+        wait("v", "est", 64)
+        if whole:
+            inc(V.tensor_tensor(T.lq[:, 0:EW], T.eq[:], T.pq[:], AluOpType.is_le), "vs", 1)
+            vsync()
+            inc(V.tensor_tensor(T.lq[:, 0:EW], T.lq[:, 0:EW], T.dq[:, 0:EW], AluOpType.mult), "vs", 1)
+            vsync()
+            inc(V.tensor_tensor(T.lq[:, 0:EW], T.eq[:], T.lq[:, 0:EW], AluOpType.max), "vs", 1)
+            vsync()
+            inc(V.tensor_copy(T.fq[:, 0:EW], T.lq[:, 0:EW]), "pf", 1)
+            wait("s", "pf", 1)
+            inc(S.dma_start(T.ena[:], T.fq[:, 0:EW]), "ero", 16)
+        else:
+            for j in range(4):
+                for a, b in (("eq", "ev"), ("pq", "pv")):
+                    inc(V.tensor_scalar(T[b][:, EW * j:EW * j + EW], T[a][:], QU * j, QU * j + QU, AluOpType.max,
+                                        AluOpType.min), "vs", 1)
+            vsync()
+            inc(V.tensor_tensor(T.eq[:], T.eq[:], T.pq[:], AluOpType.is_le), "vs", 1)
+            inc(V.tensor_tensor(T.lq[:], T.ev[:], T.pv[:], AluOpType.is_le), "vs", 1)
+            vsync()
+            inc(V.tensor_tensor(T.eq[:], T.eq[:], T.zq[:], AluOpType.mult), "vs", 1)
+            inc(V.tensor_tensor(T.lq[:], T.lq[:], T.dq[:], AluOpType.mult), "vs", 1)
+            vsync()
+            inc(V.tensor_tensor(T.lq[:], T.lq[:], T.ev[:], AluOpType.max), "vs", 1)
+            vsync()
+            inc(V.tensor_tensor(T.lq[:, 0:EW], T.lq[:, 0:EW], T.eq[:], AluOpType.max), "vs", 1)
+            vsync()
+            inc(V.tensor_tensor(T.lq[:], T.lq[:], T.lo[:], AluOpType.subtract), "vs", 1)
+            vsync()
+            inc(V.tensor_copy(T.fq[:], T.lq[:]), "pf", 1)
+            wait("s", "pf", 1)
+            for j in range(4):
+                inc(S.dma_start(T.enb[32 * j:32 * j + 32, :], T.fq[:, EW * j:EW * j + EW]), "ero", 16)
+
+    if kind:
+        if kind == "i":
+            hear("g", "fwi")
+            hear("s", "fwi")
+            inc(S.dma_start(T.img[owner], T.fwi[:]), "own", 16)
+            src, dst, rs = T.fwi[:], T.img[owner], "il"
+        else:
+            wait("g", "ero", total["ero"])
+            src, dst, rs = ((T.ena[:], T.ea[owner], "ea") if owner < WHOLE else
+                            (T.enb[:], T.eb[owner - WHOLE], "eb"))
+        fused([(m, ds, rs, [src], [dst for d in ds]) for m, ds in P["posts"][core][2]])
+
+    inc(V.memset(T.win[:, 0:PAD], -BIG), "vs", 1)
+    inc(V.memset(T.win[:, PAD + R:WIN], -BIG), "vs", 1)
+    inc(V.memset(T.neg[:], -BIG), "vs", 1)
+    inc(V.memset(T.flag[:], BIG), "vs", 1)
+    inc(V.memset(T.run[:, LIST:FA], 0.0), "vs", 1)
+    inc(V.memset(T.run[:, FA + QU:FA + ZB], -BIG), "vs", 1)
+    inc(V.memset(T.run[:, FA + ZB:FA + FB], 0.0), "vs", 1)
+    fills = total["vs"]
+
+    if is_root:
+        total["lw"] = bits(topo.mask(core, team[ROLES[NB - 2]]))
+        wait("y", "lw", total["lw"])
+        src = T.tab[GR * block:GR * block + GR, :]
+    else:
+        hear("y", "wb", bits(topo.mask(root, core)))
+        src = T.wsrc[:]
+    for k in range(8):
+        if k >= DEEP_WIN:
+            wait("y", "wl%d" % (k - DEEP_WIN), 16)
+        inc(Y.dma_start(T.win[16 * k:16 * k + 16, PAD:PAD + R], src), "wl%d" % k, 16)
+
+    if kind == "i":
+        hear("s", "il")
+        wait("s", "own", 16)
+        inc(S.dma_start(T.lt[:, 0:IW], T.img[0:WHOLE]), "irp", 16)
+        inc(S.dma_start(T.lt[0:64, IW:OW], T.img[WHOLE]), "irp", 16)
+        inc(S.dma_start(T.lt[64:128, IW:OW], T.img[WHOLE + 1]), "irp", 16)
+        wait("v", "irp", 48)
+        off_sem = inc(V.tensor_scalar(T.off[:], T.lt[:], PAD - R * owner, PAD + R, AluOpType.add, AluOpType.min),
+                      "pf", 1)
+        wait("g", *off_sem)
+        ds = [d for d in team.values() if d != core and topo.die(d) == topo.die(core)]
+        fused([(common(ds), ds, "of", [T.off[:]], [T.off[:] for d in ds])])
+    else:
+        hub = [team[r] for r in POSTS["i"] if topo.die(team[r]) == topo.die(core)][0]
+        total["of"] = bits(P["common"](hub, [d for d in team.values() if d != hub and topo.die(d) == topo.die(hub)]))
+        off_sem = ("of", total["of"])
+    for p, buf, at in (("A", "ea", 0), ("B", "eb", EW)):
+        hear("s", buf)
+        inc(S.dma_start(T.foff[:, at:at + EW], T[buf][:]), "er" + p, 16)
+
+    def ready(q):
+        wait(q, *off_sem)
+        for k in range(8):
+            wait(q, "wl%d" % k, 16)
+
+    row, a = [], 0
+    for w, q in (PIECES_EARLY if early else PIECES):
+        row.append((a, a + w, q))
+        a += w
+    got = {}
+
+    def operands(a, b, at):
+        return (T.got[:, at + a:at + b], T.win[:].indirect(T.off[:, (at + a) // 16:(at + b) // 16]))
+
+    wait("s", "vs", fills)
+    ready("s")
+    for k, (a, b, q) in enumerate(row):
+        if q == "S":
+            got[k] = inc(S.activation(*operands(a, b, 0), ActivationFunctionType.Copy), unique(), 1)
+
+    def flags(p):
+        sl, fa, fb = (slice(0, EW), 0, FA) if p == "A" else (slice(EW, 2 * EW), FA, FA + FB)
+        wait("v", "er" + p, 16)
+        inc(V.tensor_scalar(T.xoff[:, sl], T.foff[:, sl], -1, None, AluOpType.add), "vs", 1)
+        vsync()
+        inc(V.tensor_copy(T.flag[:, fa:fb].indirect(T.foff[:, sl]), T.neg[:]), "vs", 1)
+
+    def vgather(a, b, at):
+        ready("v")
+        vsync()
+        inc(V.tensor_copy(*operands(a, b, at)), "vs", 1)
+
+    def scan(a, b, base, at):
+        vsync()
+        init = T.neg[:, 0:1] if a == 0 else T.run[:, base + a - 1:base + a]
+        inc(V.tensor_tensor_scan(T.run[:, base + a:base + b], T.flag[:, base + a:base + b], T.got[:, at + a:at + b],
+                                 init, AluOpType.min, AluOpType.max), "vs", 1)
+
+    def bags(p, a, b):
+        base, end, at = (0, FA, 0) if p == "A" else (FA, FA + FB, EW)
+        return T.run[:, base:end].indirect(T.xoff[:, at + a // 16:at + b // 16])
+
+    def sources(q):
+        return [T.pa[q]] if q < WHOLE else [T.pb[4 * (q - WHOLE) + j] for j in range(4)]
+
+    def store(p, sems):
+        at = 0 if p == "A" else BAGS
+        for s in sems:
+            wait("y", *s)
+        inc(Y.dma_start(T["pa" if p == "A" else "pb"][:], T.part[:, at:at + BAGS]), "st" + p, 16)
+
+    flags("A")
+    flags("B")
+    vgather(0, QU, LIST)
+    for a, b, q in row:
+        if q == "V":
+            vgather(a, b, 0)
+    scan(0, QU, FA, LIST)
+    vsync()
+    store("B", [inc(V.tensor_copy(T.part[:, BAGS:2 * BAGS], bags("B", 0, BAGS)), unique(), 1)])
+    for k, (a, b, q) in enumerate(row):
+        if q == "S":
+            wait("v", *got[k])
+        scan(a, b, 0, 0)
+    vsync()
+    h = BAGS // 2
+    s1 = inc(V.tensor_copy(T.part[:, 0:h], bags("A", 0, h)), unique(), 1)
+    wait("s", "vs", total["vs"])
+    s2 = inc(S.activation(T.part[:, h:BAGS], bags("A", h, BAGS), ActivationFunctionType.Copy), unique(), 1)
+    store("A", [s1, s2])
+
+    def deliver(p):
+        wait("g", "st" + p, 16)
+        fused([(m, [to], sem, sources(q), [T[buf][slot]]) for m, q, to, buf, slot, sem in P["out"][(core, p)]])
+
+    def forward(p):
+        if (core, "r" + p) in P["out"]:
+            hear("g", "rl" + p)
+            fused([(m, [to], sem, [T.rl[q]], [T[buf][slot]]) for m, q, to, buf, slot, sem in P["out"][(core, "r" + p)]])
+
+    def fold(buf, k):
+        hear("g", buf)
+        srcs = [T[buf][o] for o in range(n) if o != owner or buf == "fr"]
+        if buf == "fl":
+            srcs = srcs + sources(owner)
+        fused([(topo.mask(core, root), [root], "yd%d" % k, srcs, [T.yd[k]])])
+
+    if role == RELAY["root"]:
+        deliver("B")
+        forward("B")
+        deliver("A")
+        forward("A")
+    else:
+        forward("B")
+        deliver("B")
+        forward("A")
+        deliver("A")
+    if not is_root:
+        fold("fl", block)
+    if role == "aux":
+        fold("fr", NB - 1)
+
+    if is_root:
+        for k, r in enumerate(ROLES):
+            src = team["aux"] if r == "root" else team[r]
+            hear("y", "yd%d" % k, bits(topo.mask(src, core)))
+            inc(Y.dma_start(T.y[GR * k:GR * k + GR, :], T.yd[k]), "yst", 16)
+
+    for sem in sorted(total):
+        if top.get(sem, 0) < total[sem]:
+            wait("g", sem, total[sem])

@@ -24,7 +24,9 @@ FOLD_MAX = 2
 DEEP_TAB, DEEP_WIN = 2, 3
 ROLES = ["back0", "back1", "aux", "far1", "near1", "far0", "near0", "root"]
 EARLY = 3
-POSTS = {"i": ("near0", "far0"), "e": ("near1", "far1")}
+ENDS_AFTER = 3
+OWN_AFTER = 6
+POSTS = ("near0", "far0")
 RELAY = {"back0": "far0", "back1": "far1", "aux": "near0", "root": "near1"}
 
 SCRATCH = {
@@ -54,6 +56,7 @@ SCRATCH = {
     "img": ("dram", [10, 128, 32], "int32"),
     "ste": ("dram", [128, EF], "int32"),
     "fwe": ("dram", [128, EF], "int32"),
+    "fwb": ("dram", [128, 16], "uint16"),
     "ena": ("dram", [128, 4], "uint16"),
     "enb": ("dram", [128, 16], "uint16"),
     "ea": ("dram", [8, 128, 4], "uint16"),
@@ -66,8 +69,9 @@ SCRATCH = {
     "yd": ("dram", [NB, 128, 64], "bfloat16"),
 }
 SEMAPHORES = (["ld%d" % c for c in range(NB - 1)] + ["wl%d" % c for c in range(8)] + ["yd%d" % c for c in range(NB)]
-              + ["wb", "ls", "lw", "own", "ist", "est", "ero", "fwi", "fwe", "il", "irp", "ea", "eb", "erA", "erB", "of",
-                 "rlA", "rlB", "fl", "fr", "iot", "vm", "vs", "pf", "stA", "stB", "yst"] + ["u%d" % k for k in range(12)])
+              + ["wb", "ls", "lw", "own", "ist", "ste", "est", "ero", "fwi", "fwe", "il", "irp", "ea", "eb", "erA",
+                 "erB", "of", "rlA", "rlB", "fl", "fr", "iot", "vm", "vs", "pf", "stA", "stB", "yst"]
+              + ["u%d" % k for k in range(12)])
 PIECES = [(512, "V"), (1088, "S"), (1024, "S"), (896, "S"), (576, "S")]
 PIECES_EARLY = [(1152, "S"), (1088, "S"), (1088, "S"), (768, "S")]
 PLANS = {}
@@ -131,22 +135,23 @@ def make_plan(T, topo):
         return [out[j] for j in range(len(dsts))]
 
     posts = {}
+    to_posts = {}
     for q in range(n):
         t = team[q]
+        to_posts[t["root"]] = split_mask(common(t["root"], [t[r] for r in POSTS]), 4)[0]
         for kind in "ie":
             for j in range(2):
-                src, other = t[POSTS[kind][j]], t[POSTS[kind][1 - j]]
-                m = common(t["root"], [src, other])
-                heard[(src, "fw" + kind)] = bits(m)
+                src, other = t[POSTS[j]], t[POSTS[1 - j]]
+                heard[(src, "fw" + kind)] = bits(to_posts[t["root"]])
                 if kind == "i":
-                    ds = [team[o][POSTS[kind][j]] for o in range(n) if o != q]
+                    ds = [team[o][POSTS[j]] for o in range(n) if o != q]
                     sem = "il"
                 else:
                     ds = [d for d in place if topo.die(d) == topo.die(src) and d != src] + [other]
                     sem = "ea" if q < WHOLE else "eb"
                 k = -(-len(ds) // 16)
-                posts[src] = (kind, q, list(zip(split_mask(common(src, ds), k), [ds[a::k] for a in range(k)])))
-                for m, some in posts[src][2]:
+                posts[(src, kind)] = list(zip(split_mask(common(src, ds), k), [ds[a::k] for a in range(k)]))
+                for m, some in posts[(src, kind)]:
                     for d in some:
                         heard[(d, sem)] = heard.get((d, sem), 0) + bits(m)
     out = {}
@@ -171,8 +176,8 @@ def make_plan(T, topo):
     for key in out:
         for m, q, to, buf, slot, sem in out[key]:
             heard[(to, sem)] = heard.get((to, sem), 0) + bits(m)
-    PLANS["p"] = {"cores": cores, "n": n, "team": team, "place": place, "posts": posts, "out": out, "heard": heard,
-                  "common": common}
+    PLANS["p"] = {"cores": cores, "n": n, "team": team, "place": place, "posts": posts, "to_posts": to_posts,
+                  "out": out, "heard": heard, "common": common}
     return PLANS["p"]
 
 
@@ -186,6 +191,9 @@ def rank_program(g, core, T, topo):
     team = P["team"][owner]
     root = team["root"]
     is_root = core == root
+    is_post = role in POSTS
+    whole = owner < WHOLE
+    maker = is_post if whole else is_root
     early = block < EARLY
     V, S, Y = g.vector, g.scalar, g.sync
     queues = {"g": g, "v": V, "s": S, "y": Y}
@@ -230,29 +238,14 @@ def rank_program(g, core, T, topo):
 
     common = lambda ds: P["common"](core, ds)
 
-    if is_root:
-        inc(S.dma_start(T.ste[:], T.end[:]), "est", 16)
-        if owner < WHOLE:
-            inc(Y.dma_start(T.sti[:], T.idx[:]), "ist", 16)
-        else:
-            for j in range(4):
-                inc(Y.dma_start(T.sti[32 * j:32 * j + 32, :], T.idx[:, QW * j:QW * j + QW]), "ist", 16)
-        for k in range(NB - 1):
-            if k >= DEEP_TAB:
-                wait("y", "ld%d" % (k - DEEP_TAB), 16)
-            inc(Y.dma_start(T.blk[k], T.tab[GR * k:GR * k + GR, :]), "ld%d" % k, 16)
-        for kind, src, dst in (("e", T.ste, T.fwe), ("i", T.sti, T.fwi)):
-            wait("g", kind + "st", total[kind + "st"])
-            ds = [team[r] for r in POSTS[kind]]
-            fused([(common(ds), ds, "fw" + kind, [src[:]], [dst[:] for d in ds])])
-        for k in range(NB - 1):
-            wait("g", "ld%d" % k, 16)
-            d = team[ROLES[k]]
-            fused([(topo.mask(core, d), [d], "wb", [T.blk[k]], [T.wsrc[:]])], "lw" if k == NB - 2 else "ls")
+    def to_posts(sem, src, dst):
+        ds = [team[r] for r in POSTS]
+        fused([(P["to_posts"][core], ds, sem, [src], [dst for d in ds])])
 
-    kind = P["posts"][core][0] if core in P["posts"] else ""
-    if kind == "e":
-        whole = owner < WHOLE
+    def pass_list(kind, src, dst, sem):
+        fused([(m, ds, sem, [src], [dst for d in ds]) for m, ds in P["posts"][(core, kind)]])
+
+    if maker:
         inc(V.memset(T.pq[0:1, :], 0), "vm", 1)
         if whole:
             inc(g.iota(T.dq[:, 0:EW], [[1, EW]], DA, EW), "iot", 1)
@@ -260,15 +253,26 @@ def rank_program(g, core, T, topo):
             inc(g.iota(T.dq[:], [[QU, 4], [1, EW]], DN, EW), "iot", 1)
             inc(g.iota(T.zq[:], [[1, EW]], DZ, EW), "iot", 1)
             inc(g.iota(T.lo[:], [[QU, 4], [0, EW]], 0, 0), "iot", 1)
-        hear("s", "fwe")
-        inc(S.dma_start(T.eq[:], T.fwe[:]), "est", 16)
-        inc(S.dma_start(T.pq[1:16, :], T.fwe[0:120, :]), "est", 16)
-        wait("s", "vm", 1)
-        inc(S.dma_start(T.pq[0:1, 1:EW - EF + 1], T.fwe[120:127, :]), "est", 16)
-        inc(S.dma_start(T.pq[0:1, EW - EF + 1:EW], T.fwe[127:128, 0:EF - 1]), "est", 16)
+    inc(V.memset(T.win[:, 0:PAD], -BIG), "vs", 1)
+    inc(V.memset(T.win[:, PAD + R:WIN], -BIG), "vs", 1)
+    if not (maker and is_root):
+        inc(V.memset(T.flag[:, 0:FA], BIG), "vs", 1)
+    if maker:
+        if whole:
+            hear("s", "fwe")
+            inc(S.dma_start(T.eq[:], T.fwe[:]), "est", 16)
+            inc(S.dma_start(T.pq[1:16, :], T.fwe[0:120, :]), "est", 16)
+            wait("s", "vm", 1)
+            inc(S.dma_start(T.pq[0:1, 1:EW - EF + 1], T.fwe[120:127, :]), "est", 16)
+            inc(S.dma_start(T.pq[0:1, EW - EF + 1:EW], T.fwe[127:128, 0:EF - 1]), "est", 16)
+        else:
+            inc(S.dma_start(T.eq[:], T.end[:]), "est", 16)
+            inc(S.dma_start(T.pq[1:16, :], T.end[0:15, :]), "est", 16)
+            wait("s", "vm", 1)
+            inc(S.dma_start(T.pq[0:1, 1:EW], T.end[15:16, 0:EW - 1]), "est", 16)
         wait("v", "vm", 1)
         wait("v", "iot", total["iot"])
-        wait("v", "est", 64)
+        wait("v", "est", total["est"])
         if whole:
             inc(V.tensor_tensor(T.lq[:, 0:EW], T.eq[:], T.pq[:], AluOpType.is_le), "vs", 1)
             vsync()
@@ -301,30 +305,53 @@ def rank_program(g, core, T, topo):
             wait("s", "pf", 1)
             for j in range(4):
                 inc(S.dma_start(T.enb[32 * j:32 * j + 32, :], T.fq[:, EW * j:EW * j + EW]), "ero", 16)
-
-    if kind:
-        if kind == "i":
-            hear("g", "fwi")
-            hear("s", "fwi")
-            inc(S.dma_start(T.img[owner], T.fwi[:]), "own", 16)
-            src, dst, rs = T.fwi[:], T.img[owner], "il"
-        else:
-            wait("g", "ero", total["ero"])
-            src, dst, rs = ((T.ena[:], T.ea[owner], "ea") if owner < WHOLE else
-                            (T.enb[:], T.eb[owner - WHOLE], "eb"))
-        fused([(m, ds, rs, [src], [dst for d in ds]) for m, ds in P["posts"][core][2]])
-
-    inc(V.memset(T.win[:, 0:PAD], -BIG), "vs", 1)
-    inc(V.memset(T.win[:, PAD + R:WIN], -BIG), "vs", 1)
+    if maker and is_root:
+        inc(V.memset(T.flag[:, 0:FA], BIG), "vs", 1)
     inc(V.memset(T.neg[:], -BIG), "vs", 1)
-    inc(V.memset(T.flag[:], BIG), "vs", 1)
+    inc(V.memset(T.flag[:, FA:FA + FB], BIG), "vs", 1)
     inc(V.memset(T.run[:, LIST:FA], 0.0), "vs", 1)
     inc(V.memset(T.run[:, FA + QU:FA + ZB], -BIG), "vs", 1)
     inc(V.memset(T.run[:, FA + ZB:FA + FB], 0.0), "vs", 1)
     fills = total["vs"]
 
     if is_root:
-        total["lw"] = bits(topo.mask(core, team[ROLES[NB - 2]]))
+        if whole:
+            inc(Y.dma_start(T.ste[:], T.end[:]), "ste", 16)
+            inc(Y.dma_start(T.sti[:], T.idx[:]), "ist", 16)
+        else:
+            for j in range(4):
+                inc(Y.dma_start(T.sti[32 * j:32 * j + 32, :], T.idx[:, QW * j:QW * j + QW]), "ist", 16)
+        for k in range(NB - 1):
+            if k >= DEEP_TAB:
+                wait("y", "ld%d" % (k - DEEP_TAB), 16)
+            inc(Y.dma_start(T.blk[k], T.tab[GR * k:GR * k + GR, :]), "ld%d" % k, 16)
+        if whole:
+            wait("g", "ste", 16)
+            to_posts("fwe", T.ste[:], T.fwe[:])
+        wait("g", "ist", total["ist"])
+        to_posts("fwi", T.sti[:], T.fwi[:])
+        for k in range(NB - 1):
+            wait("g", "ld%d" % k, 16)
+            d = team[ROLES[k]]
+            fused([(topo.mask(core, d), [d], "wb", [T.blk[k]], [T.wsrc[:]])], "lw" if k == OWN_AFTER else "ls")
+            if k == ENDS_AFTER and not whole:
+                wait("g", "ero", total["ero"])
+                to_posts("fwe", T.enb[:], T.fwb[:])
+
+    if is_post:
+        hear("g", "fwi")
+        pass_list("i", T.fwi[:], T.img[owner], "il")
+        if whole:
+            wait("g", "ero", total["ero"])
+            pass_list("e", T.ena[:], T.ea[owner], "ea")
+        else:
+            hear("g", "fwe")
+            pass_list("e", T.fwb[:], T.eb[owner - WHOLE], "eb")
+        hear("s", "fwi")
+        inc(S.dma_start(T.img[owner], T.fwi[:]), "own", 16)
+
+    if is_root:
+        total["lw"] = bits(topo.mask(core, team[ROLES[OWN_AFTER]]))
         wait("y", "lw", total["lw"])
         src = T.tab[GR * block:GR * block + GR, :]
     else:
@@ -335,7 +362,7 @@ def rank_program(g, core, T, topo):
             wait("y", "wl%d" % (k - DEEP_WIN), 16)
         inc(Y.dma_start(T.win[16 * k:16 * k + 16, PAD:PAD + R], src), "wl%d" % k, 16)
 
-    if kind == "i":
+    if is_post:
         hear("s", "il")
         wait("s", "own", 16)
         inc(S.dma_start(T.lt[:, 0:IW], T.img[0:WHOLE]), "irp", 16)
@@ -348,7 +375,7 @@ def rank_program(g, core, T, topo):
         ds = [d for d in team.values() if d != core and topo.die(d) == topo.die(core)]
         fused([(common(ds), ds, "of", [T.off[:]], [T.off[:] for d in ds])])
     else:
-        hub = [team[r] for r in POSTS["i"] if topo.die(team[r]) == topo.die(core)][0]
+        hub = [team[r] for r in POSTS if topo.die(team[r]) == topo.die(core)][0]
         total["of"] = bits(P["common"](hub, [d for d in team.values() if d != hub and topo.die(d) == topo.die(hub)]))
         off_sem = ("of", total["of"])
     for p, buf, at in (("A", "ea", 0), ("B", "eb", EW)):

from concourse.bass import DstId, RemoteDMATransfer
from concourse.mybir import AluOpType, ActivationFunctionType

R = 8192
LIST = 4096
BAGS = 512
GR = 16
NB = 8
PAD = 8
WIN = R + 2 * PAD
QU = LIST // 4
DA = LIST + 8
FA = DA + BAGS
DN, DZ = QU + 8, QU + 16 + BAGS
FB = DZ + BAGS
ZB = DZ - 8
IW, EW, QW = LIST // 16, BAGS // 16, QU // 16
OW = IW + QW
EF = BAGS // 128
BIG = 9.9999e29
WHOLE = 8
NCORES = 256
FOLD_MAX = 2
DEEP_TAB, DEEP_WIN = 2, 3
ROLES = ["back0", "back1", "aux", "far1", "near1", "far0", "near0", "root"]
EARLY = 3
ENDS_AFTER = 3
OWN_AFTER = 6
POSTS = ("near0", "far0")
RELAY = {"back0": "far0", "back1": "far1", "aux": "near0", "root": "near1"}

SCRATCH = {
    "win": ("sbuf", [128, WIN], "bfloat16"),
    "flag": ("sbuf", [128, FA + FB], "bfloat16"),
    "got": ("sbuf", [128, LIST + QU], "bfloat16"),
    "run": ("sbuf", [128, FA + FB], "bfloat16"),
    "part": ("sbuf", [128, 2 * BAGS], "bfloat16"),
    "neg": ("sbuf", [128, BAGS], "bfloat16"),
    "lt": ("sbuf", [128, OW], "int32"),
    "off": ("sbuf", [128, OW], "uint16"),
    "foff": ("sbuf", [128, 2 * EW], "uint16"),
    "xoff": ("sbuf", [128, 2 * EW], "uint16"),
    "eq": ("sbuf", [16, EW], "int32"),
    "pq": ("sbuf", [16, EW], "int32"),
    "ev": ("sbuf", [16, 4 * EW], "int32"),
    "pv": ("sbuf", [16, 4 * EW], "int32"),
    "dq": ("sbuf", [16, 4 * EW], "int32"),
    "zq": ("sbuf", [16, EW], "int32"),
    "lo": ("sbuf", [16, 4 * EW], "int32"),
    "lq": ("sbuf", [16, 4 * EW], "int32"),
    "fq": ("sbuf", [16, 4 * EW], "uint16"),
    "blk": ("dram", [NB, 128, R * GR // 128], "bfloat16"),
    "wsrc": ("dram", [128, R * GR // 128], "bfloat16"),
    "sti": ("dram", [128, 32], "int32"),
    "fwi": ("dram", [128, 32], "int32"),
    "img": ("dram", [10, 128, 32], "int32"),
    "ste": ("dram", [128, EF], "int32"),
    "fwe": ("dram", [128, EF], "int32"),
    "fwb": ("dram", [128, 16], "uint16"),
    "ena": ("dram", [128, 4], "uint16"),
    "enb": ("dram", [128, 16], "uint16"),
    "ea": ("dram", [8, 128, 4], "uint16"),
    "eb": ("dram", [2, 128, 16], "uint16"),
    "pa": ("dram", [8, 128, 64], "bfloat16"),
    "pb": ("dram", [8, 128, 64], "bfloat16"),
    "rl": ("dram", [10, 128, 64], "bfloat16"),
    "fl": ("dram", [10, 128, 64], "bfloat16"),
    "fr": ("dram", [10, 128, 64], "bfloat16"),
    "yd": ("dram", [NB, 128, 64], "bfloat16"),
}
SEMAPHORES = (["ld%d" % c for c in range(NB - 1)] + ["wl%d" % c for c in range(8)] + ["yd%d" % c for c in range(NB)]
              + ["wb", "ls", "lw", "own", "ist", "ste", "est", "ero", "fwi", "fwe", "il", "irp", "ea", "eb", "erA",
                 "erB", "of", "rlA", "rlB", "fl", "fr", "iot", "vm", "vs", "pf", "stA", "stB", "yst"]
              + ["u%d" % k for k in range(12)])
PIECES = [(512, "V"), (1088, "S"), (1024, "S"), (896, "S"), (576, "S")]
PIECES_EARLY = [(1152, "S"), (1088, "S"), (1088, "S"), (768, "S")]
PLANS = {}


def bits(mask):
    return bin(mask).count("1")


def split_mask(mask, k):
    eng = [1 << i for i in range(16) if mask >> i & 1]
    n = 1
    while n * 2 * k <= len(eng):
        n *= 2
    return [sum(eng[j * n:(j + 1) * n]) for j in range(k)]


def make_plan(T, topo):
    if "p" in PLANS:
        return PLANS["p"]
    cores = list(T.cores)
    n = len(cores)
    same_chip = lambda a, b: topo.host(a) == topo.host(b) and topo.chip(a) == topo.chip(b)
    team = []
    for c in cores:
        mine = [d for d in range(NCORES) if same_chip(c, d)]
        abroad = [d for d in range(NCORES) if not same_chip(c, d) and not topo.same_plane(c, d)][0]
        port = [d for d in mine if topo.may_write(d, abroad)]
        here = [d for d in mine if topo.die(d) == topo.die(c) and d != c]
        there = [d for d in mine if topo.die(d) != topo.die(c)]
        t = {"root": c, "aux": [d for d in here if d not in port][0]}
        for nm, ds in (("near", [d for d in here if d in port]), ("far", [d for d in there if d in port]),
                       ("back", [d for d in there if d not in port])):
            for k, d in enumerate(ds):
                t["%s%d" % (nm, k)] = d
        team.append(t)
    place = {}
    for o in range(n):
        for k, r in enumerate(ROLES):
            place[team[o][r]] = (o, k)
    heard = {}

    def common(src, ds):
        m = 0xFFFF
        for d in ds:
            m &= topo.mask(src, d)
        return m

    def masks(src, dsts):
        away = [j for j, d in enumerate(dsts) if not same_chip(src, d)]
        home = [j for j in range(len(dsts)) if j not in away]
        base = common(src, [dsts[j] for j in away])
        rest = common(src, [dsts[j] for j in home])
        if away:
            rest &= ~base
        out = {}
        for js, m in ((away, base), (home, rest)):
            if js:
                for j, one in zip(js, split_mask(m, len(js))):
                    out[j] = one
        return [out[j] for j in range(len(dsts))]

    posts = {}
    to_posts = {}
    for q in range(n):
        t = team[q]
        to_posts[t["root"]] = split_mask(common(t["root"], [t[r] for r in POSTS]), 4)[0]
        for kind in "ie":
            for j in range(2):
                src, other = t[POSTS[j]], t[POSTS[1 - j]]
                heard[(src, "fw" + kind)] = bits(to_posts[t["root"]])
                if kind == "i":
                    ds = [team[o][POSTS[j]] for o in range(n) if o != q]
                    sem = "il"
                else:
                    ds = [d for d in place if topo.die(d) == topo.die(src) and d != src] + [other]
                    sem = "ea" if q < WHOLE else "eb"
                k = -(-len(ds) // 16)
                posts[(src, kind)] = list(zip(split_mask(common(src, ds), k), [ds[a::k] for a in range(k)]))
                for m, some in posts[(src, kind)]:
                    for d in some:
                        heard[(d, sem)] = heard.get((d, sem), 0) + bits(m)
    out = {}
    for d in place:
        o, k = place[d]
        r = ROLES[k]
        for p, qs in (("A", range(WHOLE)), ("B", range(WHOLE, n))):
            sends, later = [], []
            for q in qs:
                to = (team[q]["aux"], "fr", o, "fr") if r == "root" else (team[q][r], "fl", o, "fl")
                if to[0] == d:
                    continue
                if topo.may_write(d, to[0]):
                    sends.append((q,) + to)
                else:
                    sends.append((q, team[o][RELAY[r]], "rl", q, "rl" + p))
                    later.append((q,) + to)
            out[(d, p)] = [(m,) + s for m, s in zip(masks(d, [s[1] for s in sends]), sends)]
            if later:
                via = team[o][RELAY[r]]
                out[(via, "r" + p)] = [(m,) + s for m, s in zip(masks(via, [s[1] for s in later]), later)]
    for key in out:
        for m, q, to, buf, slot, sem in out[key]:
            heard[(to, sem)] = heard.get((to, sem), 0) + bits(m)
    PLANS["p"] = {"cores": cores, "n": n, "team": team, "place": place, "posts": posts, "to_posts": to_posts,
                  "out": out, "heard": heard, "common": common}
    return PLANS["p"]


def rank_program(g, core, T, topo):
    P = make_plan(T, topo)
    if core not in P["place"]:
        return
    cores, n = P["cores"], P["n"]
    owner, block = P["place"][core]
    role = ROLES[block]
    team = P["team"][owner]
    root = team["root"]
    is_root = core == root
    is_post = role in POSTS
    whole = owner < WHOLE
    maker = is_post if whole else is_root
    early = block < EARLY
    V, S, Y = g.vector, g.scalar, g.sync
    queues = {"g": g, "v": V, "s": S, "y": Y}
    total, seen, top = {}, {}, {}
    fresh = [0]

    def inc(call, sem, k):
        call.then_inc(T.sem[sem], k)
        total[sem] = total.get(sem, 0) + k
        return (sem, total[sem])

    def unique():
        fresh[0] += 1
        return "u%d" % (fresh[0] - 1)

    def wait(q, sem, val):
        if seen.get((q, sem), 0) >= val:
            return
        seen[(q, sem)] = val
        top[sem] = max(top.get(sem, 0), val)
        queues[q].wait_ge(T.sem[sem], val)

    def hear(q, sem, val=None):
        total[sem] = P["heard"][(core, sem)] if val is None else val
        wait(q, sem, total[sem])

    def vsync():
        if total.get("vs", 0):
            wait("v", "vs", total["vs"])

    def dst_id(d):
        rid, pid = topo.addr(d, core)
        return DstId(rid=rid, pnc=pid)

    def fused(items, local="ls"):
        tr = []
        for m, ds, sem, srcs, dsts in items:
            tr.append(RemoteDMATransfer(dst_ids=[dst_id(d) for d in ds], dma_engine_mask=m, remote_sem=T.sem[sem],
                                        srcs=srcs, dsts=dsts, alu_op=FOLD_MAX if len(srcs) > 1 else 0))
            total[local] = total.get(local, 0) + bits(m)
        g.remote_dma_fused(tr, local_sem=T.sem[local])

    common = lambda ds: P["common"](core, ds)

    def to_posts(sem, src, dst):
        ds = [team[r] for r in POSTS]
        fused([(P["to_posts"][core], ds, sem, [src], [dst for d in ds])])

    def pass_list(kind, src, dst, sem):
        fused([(m, ds, sem, [src], [dst for d in ds]) for m, ds in P["posts"][(core, kind)]])

    if maker:
        inc(V.memset(T.pq[0:1, :], 0), "vm", 1)
        if whole:
            inc(g.iota(T.dq[:, 0:EW], [[1, EW]], DA, EW), "iot", 1)
        else:
            inc(g.iota(T.dq[:], [[QU, 4], [1, EW]], DN, EW), "iot", 1)
            inc(g.iota(T.zq[:], [[1, EW]], DZ, EW), "iot", 1)
            inc(g.iota(T.lo[:], [[QU, 4], [0, EW]], 0, 0), "iot", 1)
    inc(V.memset(T.win[:, 0:PAD], -BIG), "vs", 1)
    inc(V.memset(T.win[:, PAD + R:WIN], -BIG), "vs", 1)
    if not (maker and is_root):
        inc(V.memset(T.flag[:, 0:FA], BIG), "vs", 1)
    if maker:
        if whole:
            hear("s", "fwe")
            inc(S.dma_start(T.eq[:], T.fwe[:]), "est", 16)
            inc(S.dma_start(T.pq[1:16, :], T.fwe[0:120, :]), "est", 16)
            wait("s", "vm", 1)
            inc(S.dma_start(T.pq[0:1, 1:EW - EF + 1], T.fwe[120:127, :]), "est", 16)
            inc(S.dma_start(T.pq[0:1, EW - EF + 1:EW], T.fwe[127:128, 0:EF - 1]), "est", 16)
        else:
            inc(S.dma_start(T.eq[:], T.end[:]), "est", 16)
            inc(S.dma_start(T.pq[1:16, :], T.end[0:15, :]), "est", 16)
            wait("s", "vm", 1)
            inc(S.dma_start(T.pq[0:1, 1:EW], T.end[15:16, 0:EW - 1]), "est", 16)
        wait("v", "vm", 1)
        wait("v", "iot", total["iot"])
        wait("v", "est", total["est"])
        if whole:
            inc(V.tensor_tensor(T.lq[:, 0:EW], T.eq[:], T.pq[:], AluOpType.is_le), "vs", 1)
            vsync()
            inc(V.tensor_tensor(T.lq[:, 0:EW], T.lq[:, 0:EW], T.dq[:, 0:EW], AluOpType.mult), "vs", 1)
            vsync()
            inc(V.tensor_tensor(T.lq[:, 0:EW], T.eq[:], T.lq[:, 0:EW], AluOpType.max), "vs", 1)
            vsync()
            inc(V.tensor_copy(T.fq[:, 0:EW], T.lq[:, 0:EW]), "pf", 1)
            wait("s", "pf", 1)
            inc(S.dma_start(T.ena[:], T.fq[:, 0:EW]), "ero", 16)
        else:
            for j in range(4):
                for a, b in (("eq", "ev"), ("pq", "pv")):
                    inc(V.tensor_scalar(T[b][:, EW * j:EW * j + EW], T[a][:], QU * j, QU * j + QU, AluOpType.max,
                                        AluOpType.min), "vs", 1)
            vsync()
            inc(V.tensor_tensor(T.eq[:], T.eq[:], T.pq[:], AluOpType.is_le), "vs", 1)
            inc(V.tensor_tensor(T.lq[:], T.ev[:], T.pv[:], AluOpType.is_le), "vs", 1)
            vsync()
            inc(V.tensor_tensor(T.eq[:], T.eq[:], T.zq[:], AluOpType.mult), "vs", 1)
            inc(V.tensor_tensor(T.lq[:], T.lq[:], T.dq[:], AluOpType.mult), "vs", 1)
            vsync()
            inc(V.tensor_tensor(T.lq[:], T.lq[:], T.ev[:], AluOpType.max), "vs", 1)
            vsync()
            inc(V.tensor_tensor(T.lq[:, 0:EW], T.lq[:, 0:EW], T.eq[:], AluOpType.max), "vs", 1)
            vsync()
            inc(V.tensor_tensor(T.lq[:], T.lq[:], T.lo[:], AluOpType.subtract), "vs", 1)
            vsync()
            inc(V.tensor_copy(T.fq[:], T.lq[:]), "pf", 1)
            wait("s", "pf", 1)
            for j in range(4):
                inc(S.dma_start(T.enb[32 * j:32 * j + 32, :], T.fq[:, EW * j:EW * j + EW]), "ero", 16)
    if maker and is_root:
        inc(V.memset(T.flag[:, 0:FA], BIG), "vs", 1)
    inc(V.memset(T.neg[:], -BIG), "vs", 1)
    inc(V.memset(T.flag[:, FA:FA + FB], BIG), "vs", 1)
    inc(V.memset(T.run[:, LIST:FA], 0.0), "vs", 1)
    inc(V.memset(T.run[:, FA + QU:FA + ZB], -BIG), "vs", 1)
    inc(V.memset(T.run[:, FA + ZB:FA + FB], 0.0), "vs", 1)
    fills = total["vs"]

    if is_root:
        if whole:
            inc(Y.dma_start(T.ste[:], T.end[:]), "ste", 16)
            inc(Y.dma_start(T.sti[:], T.idx[:]), "ist", 16)
        else:
            for j in range(4):
                inc(Y.dma_start(T.sti[32 * j:32 * j + 32, :], T.idx[:, QW * j:QW * j + QW]), "ist", 16)
        for k in range(NB - 1):
            if k >= DEEP_TAB:
                wait("y", "ld%d" % (k - DEEP_TAB), 16)
            inc(Y.dma_start(T.blk[k], T.tab[GR * k:GR * k + GR, :]), "ld%d" % k, 16)
        if whole:
            wait("g", "ste", 16)
            to_posts("fwe", T.ste[:], T.fwe[:])
        wait("g", "ist", total["ist"])
        to_posts("fwi", T.sti[:], T.fwi[:])
        for k in range(NB - 1):
            wait("g", "ld%d" % k, 16)
            d = team[ROLES[k]]
            fused([(topo.mask(core, d), [d], "wb", [T.blk[k]], [T.wsrc[:]])], "lw" if k == OWN_AFTER else "ls")
            if k == ENDS_AFTER and not whole:
                wait("g", "ero", total["ero"])
                to_posts("fwe", T.enb[:], T.fwb[:])

    if is_post:
        hear("g", "fwi")
        pass_list("i", T.fwi[:], T.img[owner], "il")
        if whole:
            wait("g", "ero", total["ero"])
            pass_list("e", T.ena[:], T.ea[owner], "ea")
        else:
            hear("g", "fwe")
            pass_list("e", T.fwb[:], T.eb[owner - WHOLE], "eb")
        hear("s", "fwi")
        inc(S.dma_start(T.img[owner], T.fwi[:]), "own", 16)

    if is_root:
        total["lw"] = bits(topo.mask(core, team[ROLES[OWN_AFTER]]))
        wait("y", "lw", total["lw"])
        src = T.tab[GR * block:GR * block + GR, :]
    else:
        hear("y", "wb", bits(topo.mask(root, core)))
        src = T.wsrc[:]
    for k in range(8):
        if k >= DEEP_WIN:
            wait("y", "wl%d" % (k - DEEP_WIN), 16)
        inc(Y.dma_start(T.win[16 * k:16 * k + 16, PAD:PAD + R], src), "wl%d" % k, 16)

    if is_post:
        hear("s", "il")
        wait("s", "own", 16)
        inc(S.dma_start(T.lt[:, 0:IW], T.img[0:WHOLE]), "irp", 16)
        inc(S.dma_start(T.lt[0:64, IW:OW], T.img[WHOLE]), "irp", 16)
        inc(S.dma_start(T.lt[64:128, IW:OW], T.img[WHOLE + 1]), "irp", 16)
        wait("v", "irp", 48)
        off_sem = inc(V.tensor_scalar(T.off[:], T.lt[:], PAD - R * owner, PAD + R, AluOpType.add, AluOpType.min),
                      "pf", 1)
        wait("g", *off_sem)
        ds = [d for d in team.values() if d != core and topo.die(d) == topo.die(core)]
        fused([(common(ds), ds, "of", [T.off[:]], [T.off[:] for d in ds])])
    else:
        hub = [team[r] for r in POSTS if topo.die(team[r]) == topo.die(core)][0]
        total["of"] = bits(P["common"](hub, [d for d in team.values() if d != hub and topo.die(d) == topo.die(hub)]))
        off_sem = ("of", total["of"])
    for p, buf, at in (("A", "ea", 0), ("B", "eb", EW)):
        hear("s", buf)
        inc(S.dma_start(T.foff[:, at:at + EW], T[buf][:]), "er" + p, 16)

    def ready(q):
        wait(q, *off_sem)
        for k in range(8):
            wait(q, "wl%d" % k, 16)

    row, a = [], 0
    for w, q in (PIECES_EARLY if early else PIECES):
        row.append((a, a + w, q))
        a += w
    got = {}

    def operands(a, b, at):
        return (T.got[:, at + a:at + b], T.win[:].indirect(T.off[:, (at + a) // 16:(at + b) // 16]))

    wait("s", "vs", fills)
    ready("s")
    for k, (a, b, q) in enumerate(row):
        if q == "S":
            got[k] = inc(S.activation(*operands(a, b, 0), ActivationFunctionType.Copy), unique(), 1)

    def flags(p):
        sl, fa, fb = (slice(0, EW), 0, FA) if p == "A" else (slice(EW, 2 * EW), FA, FA + FB)
        wait("v", "er" + p, 16)
        inc(V.tensor_scalar(T.xoff[:, sl], T.foff[:, sl], -1, None, AluOpType.add), "vs", 1)
        vsync()
        inc(V.tensor_copy(T.flag[:, fa:fb].indirect(T.foff[:, sl]), T.neg[:]), "vs", 1)

    def vgather(a, b, at):
        ready("v")
        vsync()
        inc(V.tensor_copy(*operands(a, b, at)), "vs", 1)

    def scan(a, b, base, at):
        vsync()
        init = T.neg[:, 0:1] if a == 0 else T.run[:, base + a - 1:base + a]
        inc(V.tensor_tensor_scan(T.run[:, base + a:base + b], T.flag[:, base + a:base + b], T.got[:, at + a:at + b],
                                 init, AluOpType.min, AluOpType.max), "vs", 1)

    def bags(p, a, b):
        base, end, at = (0, FA, 0) if p == "A" else (FA, FA + FB, EW)
        return T.run[:, base:end].indirect(T.xoff[:, at + a // 16:at + b // 16])

    def sources(q):
        return [T.pa[q]] if q < WHOLE else [T.pb[4 * (q - WHOLE) + j] for j in range(4)]

    def store(p, sems):
        at = 0 if p == "A" else BAGS
        for s in sems:
            wait("y", *s)
        inc(Y.dma_start(T["pa" if p == "A" else "pb"][:], T.part[:, at:at + BAGS]), "st" + p, 16)

    flags("A")
    flags("B")
    vgather(0, QU, LIST)
    for a, b, q in row:
        if q == "V":
            vgather(a, b, 0)
    scan(0, QU, FA, LIST)
    vsync()
    store("B", [inc(V.tensor_copy(T.part[:, BAGS:2 * BAGS], bags("B", 0, BAGS)), unique(), 1)])
    for k, (a, b, q) in enumerate(row):
        if q == "S":
            wait("v", *got[k])
        scan(a, b, 0, 0)
    vsync()
    h = BAGS // 2
    s1 = inc(V.tensor_copy(T.part[:, 0:h], bags("A", 0, h)), unique(), 1)
    wait("s", "vs", total["vs"])
    s2 = inc(S.activation(T.part[:, h:BAGS], bags("A", h, BAGS), ActivationFunctionType.Copy), unique(), 1)
    store("A", [s1, s2])

    def deliver(p):
        wait("g", "st" + p, 16)
        fused([(m, [to], sem, sources(q), [T[buf][slot]]) for m, q, to, buf, slot, sem in P["out"][(core, p)]])

    def forward(p):
        if (core, "r" + p) in P["out"]:
            hear("g", "rl" + p)
            fused([(m, [to], sem, [T.rl[q]], [T[buf][slot]]) for m, q, to, buf, slot, sem in P["out"][(core, "r" + p)]])

    def fold(buf, k):
        hear("g", buf)
        srcs = [T[buf][o] for o in range(n) if o != owner or buf == "fr"]
        if buf == "fl":
            srcs = srcs + sources(owner)
        fused([(topo.mask(core, root), [root], "yd%d" % k, srcs, [T.yd[k]])])

    if role == RELAY["root"]:
        deliver("B")
        forward("B")
        deliver("A")
        forward("A")
    else:
        forward("B")
        deliver("B")
        forward("A")
        deliver("A")
    if not is_root:
        fold("fl", block)
    if role == "aux":
        fold("fr", NB - 1)

    if is_root:
        for k, r in enumerate(ROLES):
            src = team["aux"] if r == "root" else team[r]
            hear("y", "yd%d" % k, bits(topo.mask(src, core)))
            inc(Y.dma_start(T.y[GR * k:GR * k + GR, :], T.yd[k]), "yst", 16)

    for sem in sorted(total):
        if top.get(sem, 0) < total[sem]:
            wait("g", sem, total[sem])
